import numpy as np
import ml_dtypes


def mxq(x, axis, fmt="e4m3"):
    dtype, down = {"e4m3": (ml_dtypes.float8_e4m3fn, 7), "e5m2": (ml_dtypes.float8_e5m2, 14)}[fmt]
    v = np.moveaxis(np.asarray(x, np.float32).astype(ml_dtypes.bfloat16).astype(np.float64), axis, -1)
    blocks = v.reshape(v.shape[:-1] + (-1, 32))
    amax = np.abs(blocks).max(-1, keepdims=True)
    byte = np.maximum(np.where(amax > 0, np.frexp(amax)[1] - 1 + 127, 0) - down, 1)
    scale = np.exp2(byte - 127.0)
    codes = (blocks / scale).astype(np.float32).astype(dtype).astype(np.float64)
    return np.moveaxis((codes * scale).reshape(v.shape), -1, axis)


WIDE = False


def mx_kscale(k):
    if not WIDE:
        return np.ones(k)
    levels = np.array([10, -10, 5, -5, 0])
    if k % 512:
        return np.exp2(np.random.permutation(np.resize(levels, k // 32))).repeat(32)
    a = np.empty((k // 512, 16))
    for p in range(k // 512):
        a[p, :8] = np.random.permutation(np.resize(levels, 8))
        for g in range(8):
            far = levels[np.abs(levels - a[p, g]) >= 10]
            a[p, g + 8] = far[np.random.randint(len(far))]
    return np.exp2(a.ravel()).repeat(32)


def f64(x):
    return np.asarray(x).astype(np.float64)


def striped(idx):
    return np.tile(np.asarray(idx).reshape(-1, 16).T, (8, 1)).astype(np.uint16)


def unstriped(offs):
    return offs[:16].T.reshape(-1).astype(np.int64)


B, N, C, D, NQ = 1, 512, 2048, 1024, 256


def eight(codes):
    return np.concatenate([codes[h].reshape(-1, 16).T for h in range(8)]).astype(np.uint16)


def uneight(offs):
    return np.stack([offs[16 * h:16 * h + 16].T.reshape(-1) for h in range(8)]).astype(np.int64)


def setup_inputs():
    n = np.random.standard_normal
    s = mx_kscale(D)[:, None]
    grid = lambda x: np.round(x * 32) / 32
    return {
        "qT": (n((B, D, NQ)) * s / np.sqrt(D)).astype(np.float32),
        "cb": (grid(n((D, C))) / s).astype(np.float32),
        "norm": np.tile(np.random.randint(32, 129, N) / 64.0, (128, 1)).astype(np.float32),
        "bias": np.tile(n(N), (128, 1)).astype(np.float32),
        "offs": eight(np.random.randint(0, C, (8, N))),
        "offs2": eight(np.random.randint(0, C, (8, N))),
    }


def reference(qT, cb, norm, bias, offs, offs2):
    k = []
    for part, offs_ in enumerate((offs, offs2,)):
        codes = uneight(offs_)
        k += [f64(cb)[512 * part + 64 * h:512 * part + 64 * h + 64][:, codes[h]] for h in range(8)]
    k = np.concatenate(k) * f64(norm)[:1]
    a = mxq(f64(qT), 1, "e4m3").transpose(0, 2, 1) @ mxq(k, 0, "e4m3")
    a = a + f64(bias)[:1]
    return a

@@ -1,0 +1,144 @@
+from contextlib import ExitStack
+
+import concourse.mybir as mybir
+from concourse.masks import make_identity
+
+FLOPS = 2 * 256 * 512 * 1024
+
+P = 128
+NQ, N, C = 256, 512, 2048
+PASSES, PACK = 2, 4
+W = 256
+CHUNKS = N // W
+
+F32 = mybir.dt.float32
+BF16 = mybir.dt.bfloat16
+U32 = mybir.dt.uint32
+U16 = mybir.dt.uint16
+U8 = mybir.dt.uint8
+FP8X4 = mybir.dt.float8_e4m3fn_x4
+MULT = mybir.AluOpType.mult
+ADD = mybir.AluOpType.add
+
+
+def tile_attend_pq_lin_bias_kernel(tc, qT, cb, norm, bias, offs, offs2, out):
+    nc = tc.nc
+    q_rows = qT.flatten_outer_dims()
+    out_rows = out.flatten_outer_dims()
+    planes = cb.rearrange("(s p j) c -> s j p c", s=PASSES, j=PACK)
+    q_planes = q_rows.rearrange("(s p j) w -> s p j w", s=PASSES, j=PACK)
+
+    with ExitStack() as ctx:
+        keep = ctx.enter_context(tc.tile_pool(name="keep", bufs=1))
+        psum = ctx.enter_context(tc.psum_pool(name="psum", bufs=1))
+
+        lists = [keep.tile([P, N // 16], U16, name="list0"), keep.tile([P, N // 16], U16, name="list1")]
+        norm_t = keep.tile([P, N], F32, name="norm_t")
+        ident = keep.tile([P, P], F32, name="ident", align_bytes=64)
+        norm_rows = keep.tile([P, P], F32, name="norm_rows", align_bytes=64)
+        norm_col = keep.tile([P, N // P], F32, name="norm_col", align_bytes=64)
+        turned = psum.tile([P, P], F32, name="turned")
+        spread = psum.tile([P, N], F32, name="spread")
+        bias_t = keep.tile([P, N], F32, name="bias_t")
+        cb_t = [[keep.tile([P, C], F32, name=f"cb{s}{t}") for t in range(PACK)] for s in range(PASSES)]
+        q_raw = [keep.tile([P, PACK, NQ], F32, name=f"q_raw{s}") for s in range(PASSES)]
+        q_bf = [keep.tile([P, NQ, PACK], BF16, name=f"q_bf{s}", align_bytes=64) for s in range(PASSES)]
+        q_codes = [keep.tile([P, NQ], U32, name=f"q_codes{s}", align_bytes=64) for s in range(PASSES)]
+        q_scales = [keep.tile([P, NQ], U8, name=f"q_scales{s}", align_bytes=64) for s in range(PASSES)]
+        k_raw = [[keep.tile([P, PACK, W], F32, name=f"k_raw{s}{c}") for c in range(CHUNKS)] for s in range(PASSES)]
+        k_bf = [[keep.tile([P, W, PACK], BF16, name=f"k_bf{s}{c}", align_bytes=64) for c in range(CHUNKS)] for s in range(PASSES)]
+        k_codes = [[keep.tile([P, W], U32, name=f"k_codes{s}{c}", align_bytes=64) for c in range(CHUNKS)] for s in range(PASSES)]
+        k_scales = [[keep.tile([P, W], U8, name=f"k_scales{s}{c}", align_bytes=64) for c in range(CHUNKS)] for s in range(PASSES)]
+        acc = [[psum.tile([P, W], F32, name=f"acc{m}{c}") for c in range(CHUNKS)] for m in range(NQ // P)]
+        res = [[keep.tile([P, W], F32, name=f"res{m}{c}") for c in range(CHUNKS)] for m in range(NQ // P)]
+
+        def load_cb(s, t):
+            nc.sync.dma_start(out=cb_t[s][t][:], in_=planes[s, t])
+
+        nc.vector.memset(norm_rows[:], 0.0)
+        make_identity(nc, ident[:])
+        nc.sync.dma_start(out=lists[0][:], in_=offs)
+        load_cb(0, 0)
+        nc.sync.dma_start(out=norm_rows[0 : N // P, :], in_=norm[0:1, :].rearrange("o (m r) -> (o m) r", r=P))
+        nc.tensor.transpose(turned[:], norm_rows[:], ident[:])
+        nc.vector.tensor_copy(out=norm_col[:], in_=turned[:, 0 : N // P])
+        for m in range(N // P):
+            nc.tensor.transpose(spread[:, m * P : (m + 1) * P], norm_col[:, m : m + 1].to_broadcast([P, P]), ident[:])
+        nc.scalar.copy(out=norm_t[:], in_=spread[:])
+        load_cb(0, 1)
+        nc.sync.dma_start(out=lists[1][:], in_=offs2)
+        load_cb(0, 2)
+        nc.sync.dma_start(out=q_raw[0][:], in_=q_planes[0])
+        load_cb(0, 3)
+        load_cb(1, 0)
+        nc.sync.dma_start(out=q_raw[1][:], in_=q_planes[1])
+        load_cb(1, 1)
+        load_cb(1, 2)
+        load_cb(1, 3)
+        nc.sync.dma_start(out=bias_t[:], in_=bias)
+
+        def gather(s, t):
+            for c in range(CHUNKS):
+                cols = slice(c * W, (c + 1) * W)
+                nc.vector.tensor_tensor(
+                    k_raw[s][c][:, t, :],
+                    cb_t[s][t][:].indirect(lists[s][:, c * (W // 16) : (c + 1) * (W // 16)]),
+                    norm_t[:, cols],
+                    MULT,
+                )
+
+        def quantize_k(s, c):
+            nc.vector.quantize_mx(
+                out=k_codes[s][c][:].bitcast(FP8X4),
+                scales=k_scales[s][c][:],
+                in_=k_bf[s][c][:].rearrange("p n t -> p (n t)"),
+            )
+
+        def quantize_q(s):
+            nc.scalar.copy(out=q_bf[s][:], in_=q_raw[s][:].rearrange("p t n -> p n t"))
+            nc.vector.quantize_mx(
+                out=q_codes[s][:].bitcast(FP8X4),
+                scales=q_scales[s][:],
+                in_=q_bf[s][:].rearrange("p n t -> p (n t)"),
+            )
+
+        def multiply(s, c):
+            for m in range(NQ // P):
+                rows = slice(m * P, (m + 1) * P)
+                nc.tensor.matmul_mx(
+                    out=acc[m][c][:],
+                    lhsT=q_codes[s][:, rows].bitcast(FP8X4),
+                    lhsT_scale=q_scales[s][:, rows],
+                    rhs=k_codes[s][c][:].bitcast(FP8X4),
+                    rhs_scale=k_scales[s][c][:],
+                    start=(s == 0),
+                    stop=(s == PASSES - 1),
+                )
+
+        for t in range(PACK):
+            gather(0, t)
+        for c in range(CHUNKS):
+            nc.scalar.copy(out=k_bf[0][c][:], in_=k_raw[0][c][:].rearrange("p t n -> p n t"))
+        quantize_q(0)
+        quantize_q(1)
+        for c in range(CHUNKS):
+            quantize_k(0, c)
+        for c in range(CHUNKS):
+            multiply(0, c)
+
+        interleave = [nc.scalar.copy, nc.vector.tensor_copy]
+        for t in range(PACK - 1):
+            gather(1, t)
+        for c in range(CHUNKS):
+            interleave[c](out=k_bf[1][c][:, :, 0 : PACK - 1], in_=k_raw[1][c][:, 0 : PACK - 1, :].rearrange("p t n -> p n t"))
+        gather(1, PACK - 1)
+        for c in range(CHUNKS):
+            interleave[c](out=k_bf[1][c][:, :, PACK - 1], in_=k_raw[1][c][:, PACK - 1, :])
+        for c in range(CHUNKS):
+            quantize_k(1, c)
+        for c in range(CHUNKS):
+            cols = slice(c * W, (c + 1) * W)
+            multiply(1, c)
+            for m in range(NQ // P):
+                nc.vector.tensor_tensor(res[m][c][:], acc[m][c][:], bias_t[:, cols], ADD)
+                nc.sync.dma_start(out=out_rows[m * P : (m + 1) * P, cols], in_=res[m][c][:])

@@ -9,7 +9,7 @@ P = 128
 NQ, N, C = 256, 512, 2048
 PASSES, PACK = 2, 4
 W = 256
-CHUNKS = N // W
+HALVES = N // W
 
 F32 = mybir.dt.float32
 BF16 = mybir.dt.bfloat16
@@ -23,10 +23,9 @@ ADD = mybir.AluOpType.add
 
 def tile_attend_pq_lin_bias_kernel(tc, qT, cb, norm, bias, offs, offs2, out):
     nc = tc.nc
-    q_rows = qT.flatten_outer_dims()
     out_rows = out.flatten_outer_dims()
     planes = cb.rearrange("(s p j) c -> s j p c", s=PASSES, j=PACK)
-    q_planes = q_rows.rearrange("(s p j) w -> s p j w", s=PASSES, j=PACK)
+    q_planes = qT.flatten_outer_dims().rearrange("(s p j) w -> s p j w", s=PASSES, j=PACK)
 
     with ExitStack() as ctx:
         keep = ctx.enter_context(tc.tile_pool(name="keep", bufs=1))
@@ -45,100 +44,118 @@ def tile_attend_pq_lin_bias_kernel(tc, qT, cb, norm, bias, offs, offs2, out):
         q_bf = [keep.tile([P, NQ, PACK], BF16, name=f"q_bf{s}", align_bytes=64) for s in range(PASSES)]
         q_codes = [keep.tile([P, NQ], U32, name=f"q_codes{s}", align_bytes=64) for s in range(PASSES)]
         q_scales = [keep.tile([P, NQ], U8, name=f"q_scales{s}", align_bytes=64) for s in range(PASSES)]
-        k_raw = [[keep.tile([P, PACK, W], F32, name=f"k_raw{s}{c}") for c in range(CHUNKS)] for s in range(PASSES)]
-        k_bf = [[keep.tile([P, W, PACK], BF16, name=f"k_bf{s}{c}", align_bytes=64) for c in range(CHUNKS)] for s in range(PASSES)]
-        k_codes = [[keep.tile([P, W], U32, name=f"k_codes{s}{c}", align_bytes=64) for c in range(CHUNKS)] for s in range(PASSES)]
-        k_scales = [[keep.tile([P, W], U8, name=f"k_scales{s}{c}", align_bytes=64) for c in range(CHUNKS)] for s in range(PASSES)]
-        acc = [[psum.tile([P, W], F32, name=f"acc{m}{c}") for c in range(CHUNKS)] for m in range(NQ // P)]
-        res = [[keep.tile([P, W], F32, name=f"res{m}{c}") for c in range(CHUNKS)] for m in range(NQ // P)]
+        k_raw = [[keep.tile([P, PACK, W], F32, name=f"k_raw{s}{h}") for h in range(HALVES)] for s in range(PASSES)]
+        k_bf = [[keep.tile([P, W, PACK], BF16, name=f"k_bf{s}{h}", align_bytes=64) for h in range(HALVES)] for s in range(PASSES)]
+        k_codes = [[keep.tile([P, W], U32, name=f"k_codes{s}{h}", align_bytes=64) for h in range(HALVES)] for s in range(PASSES)]
+        k_scales = [[keep.tile([P, W], U8, name=f"k_scales{s}{h}", align_bytes=64) for h in range(HALVES)] for s in range(PASSES)]
+        acc = [[psum.tile([P, W], F32, name=f"acc{m}{h}") for h in range(HALVES)] for m in range(NQ // P)]
+        res = [[keep.tile([P, W], F32, name=f"res{m}{h}") for h in range(HALVES)] for m in range(NQ // P)]
 
         def load_cb(s, t):
             nc.sync.dma_start(out=cb_t[s][t][:], in_=planes[s, t])
+
+        def load_q(s):
+            nc.sync.dma_start(out=q_raw[s][:], in_=q_planes[s])
+
+        def gather(s, t, c0, c1):
+            h = c0 // W
+            nc.vector.tensor_tensor(
+                k_raw[s][h][:, t, c0 - h * W : c1 - h * W],
+                cb_t[s][t][:].indirect(lists[s][:, c0 // 16 : c1 // 16]),
+                norm_t[:, c0:c1],
+                MULT,
+            )
+
+        def interleave(copy, dst, src, t0, t1, c0, c1):
+            copy(
+                out=dst[:, c0:c1, t0:t1].rearrange("p (c i) t -> p c t i", i=4),
+                in_=src[:, t0:t1, c0:c1].rearrange("p t (c i) -> p c t i", i=4),
+            )
+
+        def quantize(codes, scales, grouped, c0, c1):
+            nc.vector.quantize_mx(
+                out=codes[:, c0:c1].bitcast(FP8X4),
+                scales=scales[:, c0:c1],
+                in_=grouped[:, c0:c1, :].rearrange("p n t -> p (n t)"),
+            )
+
+        def multiply(s, h, m):
+            rows = slice(m * P, (m + 1) * P)
+            nc.tensor.matmul_mx(
+                out=acc[m][h][:],
+                lhsT=q_codes[s][:, rows].bitcast(FP8X4),
+                lhsT_scale=q_scales[s][:, rows],
+                rhs=k_codes[s][h][:].bitcast(FP8X4),
+                rhs_scale=k_scales[s][h][:],
+                start=(s == 0),
+                stop=(s == PASSES - 1),
+            )
 
         nc.vector.memset(norm_rows[:], 0.0)
         make_identity(nc, ident[:])
         nc.sync.dma_start(out=lists[0][:], in_=offs)
         load_cb(0, 0)
         nc.sync.dma_start(out=norm_rows[0 : N // P, :], in_=norm[0:1, :].rearrange("o (m r) -> (o m) r", r=P))
+        load_cb(0, 1)
+        load_q(0)
+        load_cb(0, 2)
+        nc.sync.dma_start(out=lists[1][:], in_=offs2)
+        load_cb(0, 3)
+        for t in range(PACK):
+            load_cb(1, t)
+        load_q(1)
+        nc.sync.dma_start(out=bias_t[:], in_=bias)
+
         nc.tensor.transpose(turned[:], norm_rows[:], ident[:])
         nc.vector.tensor_copy(out=norm_col[:], in_=turned[:, 0 : N // P])
         for m in range(N // P):
             nc.tensor.transpose(spread[:, m * P : (m + 1) * P], norm_col[:, m : m + 1].to_broadcast([P, P]), ident[:])
         nc.scalar.copy(out=norm_t[:], in_=spread[:])
-        load_cb(0, 1)
-        nc.sync.dma_start(out=lists[1][:], in_=offs2)
-        load_cb(0, 2)
-        nc.sync.dma_start(out=q_raw[0][:], in_=q_planes[0])
-        load_cb(0, 3)
-        load_cb(1, 0)
-        nc.sync.dma_start(out=q_raw[1][:], in_=q_planes[1])
-        load_cb(1, 1)
-        load_cb(1, 2)
-        load_cb(1, 3)
-        nc.sync.dma_start(out=bias_t[:], in_=bias)
 
-        def gather(s, t):
-            for c in range(CHUNKS):
-                cols = slice(c * W, (c + 1) * W)
-                nc.vector.tensor_tensor(
-                    k_raw[s][c][:, t, :],
-                    cb_t[s][t][:].indirect(lists[s][:, c * (W // 16) : (c + 1) * (W // 16)]),
-                    norm_t[:, cols],
-                    MULT,
-                )
+        def work_q(s, copy):
+            interleave(copy, q_bf[s], q_raw[s], 0, PACK, 0, NQ)
 
-        def quantize_k(s, c):
-            nc.vector.quantize_mx(
-                out=k_codes[s][c][:].bitcast(FP8X4),
-                scales=k_scales[s][c][:],
-                in_=k_bf[s][c][:].rearrange("p n t -> p (n t)"),
-            )
-
-        def quantize_q(s):
-            nc.scalar.copy(out=q_bf[s][:], in_=q_raw[s][:].rearrange("p t n -> p n t"))
-            nc.vector.quantize_mx(
-                out=q_codes[s][:].bitcast(FP8X4),
-                scales=q_scales[s][:],
-                in_=q_bf[s][:].rearrange("p n t -> p (n t)"),
-            )
-
-        def multiply(s, c):
+        for t in (0, 1):
+            for h in range(HALVES):
+                gather(0, t, h * W, (h + 1) * W)
+        work_q(0, nc.scalar.copy)
+        quantize(q_codes[0], q_scales[0], q_bf[0], 0, NQ)
+        for t in (2, 3):
+            for h in range(HALVES):
+                gather(0, t, h * W, (h + 1) * W)
+        for h in range(HALVES):
+            interleave(nc.scalar.copy, k_bf[0][h], k_raw[0][h], 0, PACK, 0, W)
+        for h in range(HALVES):
+            gather(1, 0, h * W, (h + 1) * W)
+        for h in range(HALVES):
+            quantize(k_codes[0][h], k_scales[0][h], k_bf[0][h], 0, W)
+        for h in range(HALVES):
             for m in range(NQ // P):
-                rows = slice(m * P, (m + 1) * P)
-                nc.tensor.matmul_mx(
-                    out=acc[m][c][:],
-                    lhsT=q_codes[s][:, rows].bitcast(FP8X4),
-                    lhsT_scale=q_scales[s][:, rows],
-                    rhs=k_codes[s][c][:].bitcast(FP8X4),
-                    rhs_scale=k_scales[s][c][:],
-                    start=(s == 0),
-                    stop=(s == PASSES - 1),
-                )
+                multiply(0, h, m)
+        for t in (1, 2):
+            for h in range(HALVES):
+                gather(1, t, h * W, (h + 1) * W)
+        last = PACK - 1
+        interleave(nc.scalar.copy, k_bf[1][0], k_raw[1][0], 0, last, 0, P)
+        interleave(nc.vector.tensor_copy, k_bf[1][0], k_raw[1][0], 0, last, P, W)
+        interleave(nc.vector.tensor_copy, k_bf[1][1], k_raw[1][1], 0, last, 0, W)
 
-        for t in range(PACK):
-            gather(0, t)
-        for c in range(CHUNKS):
-            nc.scalar.copy(out=k_bf[0][c][:], in_=k_raw[0][c][:].rearrange("p t n -> p n t"))
-        quantize_q(0)
-        quantize_q(1)
-        for c in range(CHUNKS):
-            quantize_k(0, c)
-        for c in range(CHUNKS):
-            multiply(0, c)
-
-        interleave = [nc.scalar.copy, nc.vector.tensor_copy]
-        for t in range(PACK - 1):
-            gather(1, t)
-        for c in range(CHUNKS):
-            interleave[c](out=k_bf[1][c][:, :, 0 : PACK - 1], in_=k_raw[1][c][:, 0 : PACK - 1, :].rearrange("p t n -> p n t"))
-        gather(1, PACK - 1)
-        for c in range(CHUNKS):
-            interleave[c](out=k_bf[1][c][:, :, PACK - 1], in_=k_raw[1][c][:, PACK - 1, :])
-        for c in range(CHUNKS):
-            quantize_k(1, c)
-        for c in range(CHUNKS):
-            cols = slice(c * W, (c + 1) * W)
-            multiply(1, c)
-            for m in range(NQ // P):
-                nc.vector.tensor_tensor(res[m][c][:], acc[m][c][:], bias_t[:, cols], ADD)
-                nc.sync.dma_start(out=out_rows[m * P : (m + 1) * P, cols], in_=res[m][c][:])
+        gather(1, last, 0, P)
+        gather(1, last, P, W)
+        gather(1, last, W, N)
+        nc.scalar.copy(out=k_bf[1][0][:, 0:P, last], in_=k_raw[1][0][:, last, 0:P])
+        for m in range(NQ // P):
+            interleave(nc.scalar.copy, q_bf[1], q_raw[1], 0, PACK, m * P, (m + 1) * P)
+        nc.vector.tensor_copy(out=k_bf[1][0][:, P:W, last], in_=k_raw[1][0][:, last, P:W])
+        nc.vector.tensor_copy(out=k_bf[1][1][:, :, last], in_=k_raw[1][1][:, last, :])
+        quantize(k_codes[1][0], k_scales[1][0], k_bf[1][0], 0, W)
+        quantize(q_codes[1], q_scales[1], q_bf[1], 0, P)
+        quantize(k_codes[1][1], k_scales[1][1], k_bf[1][1], 0, W)
+        quantize(q_codes[1], q_scales[1], q_bf[1], P, NQ)
+        for m in range(NQ // P):
+            for h in range(HALVES):
+                multiply(1, h, m)
+            for h in range(HALVES):
+                cols = slice(h * W, (h + 1) * W)
+                nc.vector.tensor_tensor(res[m][h][:], acc[m][h][:], bias_t[:, cols], ADD)
+                nc.sync.dma_start(out=out_rows[m * P : (m + 1) * P, cols], in_=res[m][h][:])

from contextlib import ExitStack

import concourse.mybir as mybir
from concourse.masks import make_identity

FLOPS = 2 * 256 * 512 * 1024

P = 128
NQ, N, C = 256, 512, 2048
PASSES, PACK = 2, 4
W = 256
HALVES = N // W

F32 = mybir.dt.float32
BF16 = mybir.dt.bfloat16
U32 = mybir.dt.uint32
U16 = mybir.dt.uint16
U8 = mybir.dt.uint8
FP8X4 = mybir.dt.float8_e4m3fn_x4
MULT = mybir.AluOpType.mult
ADD = mybir.AluOpType.add


def tile_attend_pq_lin_bias_kernel(tc, qT, cb, norm, bias, offs, offs2, out):
    nc = tc.nc
    out_rows = out.flatten_outer_dims()
    planes = cb.rearrange("(s p j) c -> s j p c", s=PASSES, j=PACK)
    q_planes = qT.flatten_outer_dims().rearrange("(s p j) w -> s p j w", s=PASSES, j=PACK)

    with ExitStack() as ctx:
        keep = ctx.enter_context(tc.tile_pool(name="keep", bufs=1))
        psum = ctx.enter_context(tc.psum_pool(name="psum", bufs=1))

        lists = [keep.tile([P, N // 16], U16, name="list0"), keep.tile([P, N // 16], U16, name="list1")]
        norm_t = keep.tile([P, N], F32, name="norm_t")
        ident = keep.tile([P, P], F32, name="ident", align_bytes=64)
        norm_rows = keep.tile([P, P], F32, name="norm_rows", align_bytes=64)
        norm_col = keep.tile([P, N // P], F32, name="norm_col", align_bytes=64)
        turned = psum.tile([P, P], F32, name="turned")
        spread = psum.tile([P, N], F32, name="spread")
        bias_t = keep.tile([P, N], F32, name="bias_t")
        cb_t = [[keep.tile([P, C], F32, name=f"cb{s}{t}") for t in range(PACK)] for s in range(PASSES)]
        q_raw = [keep.tile([P, PACK, NQ], F32, name=f"q_raw{s}") for s in range(PASSES)]
        q_bf = [keep.tile([P, NQ, PACK], BF16, name=f"q_bf{s}", align_bytes=64) for s in range(PASSES)]
        q_codes = [keep.tile([P, NQ], U32, name=f"q_codes{s}", align_bytes=64) for s in range(PASSES)]
        q_scales = [keep.tile([P, NQ], U8, name=f"q_scales{s}", align_bytes=64) for s in range(PASSES)]
        k_raw = [[keep.tile([P, PACK, W], F32, name=f"k_raw{s}{h}") for h in range(HALVES)] for s in range(PASSES)]
        k_bf = [[keep.tile([P, W, PACK], BF16, name=f"k_bf{s}{h}", align_bytes=64) for h in range(HALVES)] for s in range(PASSES)]
        k_codes = [[keep.tile([P, W], U32, name=f"k_codes{s}{h}", align_bytes=64) for h in range(HALVES)] for s in range(PASSES)]
        k_scales = [[keep.tile([P, W], U8, name=f"k_scales{s}{h}", align_bytes=64) for h in range(HALVES)] for s in range(PASSES)]
        acc = [[psum.tile([P, W], F32, name=f"acc{m}{h}") for h in range(HALVES)] for m in range(NQ // P)]
        res = [[keep.tile([P, W], F32, name=f"res{m}{h}") for h in range(HALVES)] for m in range(NQ // P)]

        def load_cb(s, t):
            nc.sync.dma_start(out=cb_t[s][t][:], in_=planes[s, t])

        def load_q(s):
            nc.sync.dma_start(out=q_raw[s][:], in_=q_planes[s])

        def gather(s, t, c0, c1):
            h = c0 // W
            nc.vector.tensor_tensor(
                k_raw[s][h][:, t, c0 - h * W : c1 - h * W],
                cb_t[s][t][:].indirect(lists[s][:, c0 // 16 : c1 // 16]),
                norm_t[:, c0:c1],
                MULT,
            )

        def interleave(copy, dst, src, t0, t1, c0, c1):
            copy(
                out=dst[:, c0:c1, t0:t1].rearrange("p (c i) t -> p c t i", i=4),
                in_=src[:, t0:t1, c0:c1].rearrange("p t (c i) -> p c t i", i=4),
            )

        def quantize(codes, scales, grouped, c0, c1):
            nc.vector.quantize_mx(
                out=codes[:, c0:c1].bitcast(FP8X4),
                scales=scales[:, c0:c1],
                in_=grouped[:, c0:c1, :].rearrange("p n t -> p (n t)"),
            )

        def multiply(s, h, m):
            rows = slice(m * P, (m + 1) * P)
            nc.tensor.matmul_mx(
                out=acc[m][h][:],
                lhsT=q_codes[s][:, rows].bitcast(FP8X4),
                lhsT_scale=q_scales[s][:, rows],
                rhs=k_codes[s][h][:].bitcast(FP8X4),
                rhs_scale=k_scales[s][h][:],
                start=(s == 0),
                stop=(s == PASSES - 1),
            )

        nc.vector.memset(norm_rows[:], 0.0)
        make_identity(nc, ident[:])
        nc.sync.dma_start(out=lists[0][:], in_=offs)
        load_cb(0, 0)
        nc.sync.dma_start(out=norm_rows[0 : N // P, :], in_=norm[0:1, :].rearrange("o (m r) -> (o m) r", r=P))
        load_cb(0, 1)
        load_q(0)
        load_cb(0, 2)
        nc.sync.dma_start(out=lists[1][:], in_=offs2)
        load_cb(0, 3)
        for t in range(PACK):
            load_cb(1, t)
        load_q(1)
        nc.sync.dma_start(out=bias_t[:], in_=bias)

        nc.tensor.transpose(turned[:], norm_rows[:], ident[:])
        nc.vector.tensor_copy(out=norm_col[:], in_=turned[:, 0 : N // P])
        for m in range(N // P):
            nc.tensor.transpose(spread[:, m * P : (m + 1) * P], norm_col[:, m : m + 1].to_broadcast([P, P]), ident[:])
        nc.scalar.copy(out=norm_t[:], in_=spread[:])

        def work_q(s, copy):
            interleave(copy, q_bf[s], q_raw[s], 0, PACK, 0, NQ)

        for t in (0, 1):
            for h in range(HALVES):
                gather(0, t, h * W, (h + 1) * W)
        work_q(0, nc.scalar.copy)
        quantize(q_codes[0], q_scales[0], q_bf[0], 0, NQ)
        for t in (2, 3):
            for h in range(HALVES):
                gather(0, t, h * W, (h + 1) * W)
        for h in range(HALVES):
            interleave(nc.scalar.copy, k_bf[0][h], k_raw[0][h], 0, PACK, 0, W)
        for h in range(HALVES):
            gather(1, 0, h * W, (h + 1) * W)
        for h in range(HALVES):
            quantize(k_codes[0][h], k_scales[0][h], k_bf[0][h], 0, W)
        for h in range(HALVES):
            for m in range(NQ // P):
                multiply(0, h, m)
        for t in (1, 2):
            for h in range(HALVES):
                gather(1, t, h * W, (h + 1) * W)
        last = PACK - 1
        interleave(nc.scalar.copy, k_bf[1][0], k_raw[1][0], 0, last, 0, P)
        interleave(nc.vector.tensor_copy, k_bf[1][0], k_raw[1][0], 0, last, P, W)
        interleave(nc.vector.tensor_copy, k_bf[1][1], k_raw[1][1], 0, last, 0, W)

        gather(1, last, 0, P)
        gather(1, last, P, W)
        gather(1, last, W, N)
        nc.scalar.copy(out=k_bf[1][0][:, 0:P, last], in_=k_raw[1][0][:, last, 0:P])
        for m in range(NQ // P):
            interleave(nc.scalar.copy, q_bf[1], q_raw[1], 0, PACK, m * P, (m + 1) * P)
        nc.vector.tensor_copy(out=k_bf[1][0][:, P:W, last], in_=k_raw[1][0][:, last, P:W])
        nc.vector.tensor_copy(out=k_bf[1][1][:, :, last], in_=k_raw[1][1][:, last, :])
        quantize(k_codes[1][0], k_scales[1][0], k_bf[1][0], 0, W)
        quantize(q_codes[1], q_scales[1], q_bf[1], 0, P)
        quantize(k_codes[1][1], k_scales[1][1], k_bf[1][1], 0, W)
        quantize(q_codes[1], q_scales[1], q_bf[1], P, NQ)
        for m in range(NQ // P):
            for h in range(HALVES):
                multiply(1, h, m)
            for h in range(HALVES):
                cols = slice(h * W, (h + 1) * W)
                nc.vector.tensor_tensor(res[m][h][:], acc[m][h][:], bias_t[:, cols], ADD)
                nc.sync.dma_start(out=out_rows[m * P : (m + 1) * P, cols], in_=res[m][h][:])
